import numpy as np
import ml_dtypes


def mxq(x, axis, fmt="e4m3"):
    dtype, down = {"e4m3": (ml_dtypes.float8_e4m3fn, 7), "e5m2": (ml_dtypes.float8_e5m2, 14)}[fmt]
    v = np.moveaxis(np.asarray(x, np.float32).astype(ml_dtypes.bfloat16).astype(np.float64), axis, -1)
    blocks = v.reshape(v.shape[:-1] + (-1, 32))
    amax = np.abs(blocks).max(-1, keepdims=True)
    byte = np.maximum(np.where(amax > 0, np.frexp(amax)[1] - 1 + 127, 0) - down, 1)
    scale = np.exp2(byte - 127.0)
    codes = (blocks / scale).astype(np.float32).astype(dtype).astype(np.float64)
    return np.moveaxis((codes * scale).reshape(v.shape), -1, axis)


WIDE = False


def mx_kscale(k):
    if not WIDE:
        return np.ones(k)
    levels = np.array([10, -10, 5, -5, 0])
    if k % 512:
        return np.exp2(np.random.permutation(np.resize(levels, k // 32))).repeat(32)
    a = np.empty((k // 512, 16))
    for p in range(k // 512):
        a[p, :8] = np.random.permutation(np.resize(levels, 8))
        for g in range(8):
            far = levels[np.abs(levels - a[p, g]) >= 10]
            a[p, g + 8] = far[np.random.randint(len(far))]
    return np.exp2(a.ravel()).repeat(32)


def f64(x):
    return np.asarray(x).astype(np.float64)


def striped(idx):
    return np.tile(idx.reshape(-1, 16).T, (8, 1)).astype(np.uint16)


def unstriped(offs):
    return offs[:16].T.reshape(-1).astype(np.int64)


def pack_weight(w):
    k, n = w.shape
    w = f64(np.asarray(w, np.float32).astype(ml_dtypes.bfloat16)).reshape(k // 32, 32, n)
    amax = np.abs(w).max(1)
    byte = np.clip(np.where(amax > 0, np.frexp(amax)[1] - 1 + 127 - 7, 1), 1, 254)
    scaled = (w * np.exp2(127.0 - byte)[:, None, :]).reshape(k, n).astype(np.float32)
    words = np.ascontiguousarray(scaled.reshape(k // 512, 128, 4, n).transpose(0, 1, 3, 2)).astype(ml_dtypes.float8_e4m3fn).view(np.uint8)
    return words, np.ascontiguousarray(byte.astype(np.uint8).reshape(k // 512, 16, n))


def unpack_weight(words, scales):
    g, p, n, _ = words.shape
    vals = np.ascontiguousarray(words).view(ml_dtypes.float8_e4m3fn).astype(np.float64) * np.repeat(np.exp2(scales.astype(np.float64) - 127.0), 8, axis=1)[..., None]
    return vals.transpose(0, 1, 3, 2).reshape(g * 512, n)


K, T, S, N = 512, 1024, 512, 256
P = 2 ** 7


def setup_inputs():
    n = np.random.standard_normal
    s = mx_kscale(K)[:, None]
    packed_xT = pack_weight(n((K, T)) * s)
    return {
        "x_words": packed_xT[0],
        "x_scales": packed_xT[1],
        "w1": (n((K, N)) / np.sqrt(K) / s).astype(np.float32),
        "react": (np.random.uniform(0.0, 0.6, (N, S))).astype(np.float32),
        "res": (np.tile(np.random.uniform(0.02, 0.2, S), (P, 1))).astype(np.float32),
        "rea": (np.tile(np.random.uniform(0.02, 0.2, S), (P, 1))).astype(np.float32),
        "volt": (np.random.uniform(0.8, 1.2, (N, S))).astype(np.float32),
        "offs": striped(np.random.permutation(T)[:S]),
        "cha": striped(np.random.permutation(S)),
        "chb": striped(np.random.permutation(S)),
        "par": striped(np.random.randint(0, S, S)),
    }


def reference(x_words, x_scales, w1, react, res, rea, volt, offs, cha, chb, par):
    xq = unpack_weight(x_words, x_scales)[:, unstriped(offs)]
    y = mxq(f64(w1), 0, "e4m3").T @ xq
    load = np.log(np.exp(y) + 1.0)
    pf = load + 0.5 * (load[:, unstriped(cha)] + load[:, unstriped(chb)])
    qf = f64(react) + 0.5 * (f64(react)[:, unstriped(cha)] + f64(react)[:, unstriped(chb)])
    drop = 2.0 * (f64(res)[:1] * pf + f64(rea)[:1] * qf)
    va = f64(volt)[:, unstriped(par)] - drop
    return (f64(res)[:1] * ((pf) ** 2 + (qf) ** 2)) / (np.abs(va) + 0.3)

from contextlib import ExitStack

import concourse.mybir as mybir
from concourse.masks import make_identity

K, T, S, N = 512, 1024, 512, 256
FLOPS = 2 * K * N * S

F32 = mybir.dt.float32
BF16 = mybir.dt.bfloat16
I32 = mybir.dt.int32
U32 = mybir.dt.uint32
U16 = mybir.dt.uint16
U8 = mybir.dt.uint8
FP8X4 = mybir.dt.float8_e4m3fn_x4
ACT = mybir.ActivationFunctionType
ALU = mybir.AluOpType

P = 128
PACK = 4
BLOCKS = N // P
CHUNKS = S // P
HALVES = 2
HALF = S // HALVES
PER_HALF = CHUNKS // HALVES
LIST_COLS = HALF // 16


def tile_picked_ylindst_loss_p_kernel(
    tc, x_words, x_scales, w1, react, res, rea, volt, offs, cha, chb, par, out
):
    nc = tc.nc
    with ExitStack() as ctx:
        keep = ctx.enter_context(tc.tile_pool(name="keep", bufs=1))
        psum = ctx.enter_context(tc.psum_pool(name="psum", bufs=1))

        offs_t = keep.tile([P, S // 16], U16, name="offs_t")
        cha_t = keep.tile([P, S // 16], U16, name="cha_t")
        chb_t = keep.tile([P, S // 16], U16, name="chb_t")
        par_t = keep.tile([P, S // 16], U16, name="par_t")
        x_w = keep.tile([P, T], I32, name="x_w")
        x_s = keep.tile([P, T], U8, name="x_s")
        w_raw = [keep.tile([P, PACK, P], F32, name=f"w_raw{b}") for b in range(BLOCKS)]
        react_t = [keep.tile([P, S], F32, name=f"react{b}") for b in range(BLOCKS)]
        volt_t = [keep.tile([P, S], F32, name=f"volt{b}") for b in range(BLOCKS)]
        rows = keep.tile([P, P], F32, name="rows")
        ident = keep.tile([P, P], F32, name="ident")

        nc.gpsimd.memset(x_s[:].bitcast(I32), 0)
        nc.gpsimd.memset(rows[:], 0.0)
        make_identity(nc, ident[:])
        nc.sync.dma_start(offs_t[:], offs)
        for q in range(4):
            nc.sync.dma_start(x_s[32 * q : 32 * q + 4, :].bitcast(I32), x_scales[0, 4 * q : 4 * q + 4, :].bitcast(I32))
        nc.sync.dma_start(x_w[:], x_words[0].rearrange("p n t -> p (n t)").bitcast(I32))
        for b in range(BLOCKS):
            nc.sync.dma_start(w_raw[b][:], w1[:, b * P : (b + 1) * P].rearrange("(p t) n -> p t n", t=PACK))
        nc.sync.dma_start(react_t[0][:], react[0:P, :])
        nc.sync.dma_start(cha_t[:], cha)
        nc.sync.dma_start(chb_t[:], chb)
        nc.sync.dma_start(react_t[1][:], react[P : 2 * P, :])
        nc.sync.dma_start(rows[0:CHUNKS, :], res[0, :].rearrange("(c p) -> c p", p=P))
        nc.sync.dma_start(rows[32 : 32 + CHUNKS, :], rea[0, :].rearrange("(c p) -> c p", p=P))
        nc.sync.dma_start(par_t[:], par)
        for b in range(BLOCKS):
            nc.sync.dma_start(volt_t[b][:], volt[b * P : (b + 1) * P, :])

        def bank(tag, name):
            return psum.tile([P, S], F32, tag=tag, name=name)

        def turn(dst, src, start, stop):
            nc.tensor.matmul(dst, src, ident[:], start=start, stop=stop, is_transpose=True)

        def piece(list_t, h):
            return list_t[:, h * LIST_COLS : (h + 1) * LIST_COLS]

        def node_cols(cc, b):
            return slice((cc * BLOCKS + b) * P, (cc * BLOCKS + b + 1) * P)

        def row_cols(cc, b):
            return slice((b * PER_HALF + cc) * P, (b * PER_HALF + cc + 1) * P)

        squares = [(cc, b) for b in range(BLOCKS) for cc in range(PER_HALF)]

        def to_nodes(dst, src_of, first, last, which=squares):
            for i, (cc, b) in enumerate(which):
                turn(dst[:, node_cols(cc, b)], src_of(cc, b), first and i == 0, last and i == len(which) - 1)

        def to_rows(dst, src, first, last):
            for i, (cc, b) in enumerate(squares):
                turn(dst[:, row_cols(cc, b)], src[:, node_cols(cc, b)], first and i == 0, last and i == len(squares) - 1)

        def own(tiles, h):
            return lambda cc, b: tiles[b][:, (h * PER_HALF + cc) * P : (h * PER_HALF + cc + 1) * P]

        def fetched(tile):
            return lambda cc, b: tile[:, b, cc * P : (cc + 1) * P]

        def per_chunk(h):
            return [(h * PER_HALF + cc, slice(cc * N, (cc + 1) * N)) for cc in range(PER_HALF)]

        x_sg = keep.tile([P, S], U8, name="x_sg", align_bytes=64)
        x_wg = keep.tile([P, S], U32, name="x_wg", align_bytes=64)
        nc.vector.tensor_copy(x_sg[:], x_s[:].indirect(offs_t[:]))
        nc.vector.tensor_copy(x_wg[:], x_w[:].bitcast(U32).indirect(offs_t[:]))

        w_bf = keep.tile([P, N, PACK], BF16, name="w_bf", align_bytes=64, tag="w_bf")
        w_q = keep.tile([P, N], U32, name="w_q", align_bytes=64)
        w_s = keep.tile([P, N], U8, name="w_s", align_bytes=64)
        y = [bank(f"A{b}", f"y{b}") for b in range(BLOCKS)]
        for b in range(BLOCKS):
            cols = slice(b * P, (b + 1) * P)
            nc.scalar.copy(w_bf[:, cols, :], w_raw[b][:].rearrange("p t n -> p n t"))
            nc.vector.quantize_mx(out=w_q[:, cols].bitcast(FP8X4), scales=w_s[:, cols], in_=w_bf[:, cols, :].rearrange("p n t -> p (n t)"))
            nc.tensor.matmul_mx(
                out=y[b][:],
                lhsT=w_q[:, cols].bitcast(FP8X4),
                lhsT_scale=w_s[:, cols],
                rhs=x_wg[:].bitcast(FP8X4),
                rhs_scale=x_sg[:],
                start=True,
                stop=True,
            )

        mag = keep.tile([P, BLOCKS, S], F32, name="mag")
        small = keep.tile([P, BLOCKS, S], F32, name="small", tag="after")
        tail = keep.tile([P, BLOCKS, S], F32, name="tail")
        load = [keep.tile([P, S], F32, name=f"load{b}") for b in range(BLOCKS)]
        for b in range(BLOCKS):
            nc.scalar.activation(mag[:, b, :], y[b][:], ACT.Abs)
        nc.scalar.activation(small[:], mag[:], ACT.Exp, scale=-1.0)
        for b in range(BLOCKS):
            nc.scalar.activation(tail[:, b, :], small[:, b, :], ACT.Ln, bias=1.0)
            nc.vector.scalar_tensor_tensor(load[b][:], y[b][:], 0.0, tail[:, b, :], ALU.max, ALU.add)

        qa = keep.tile([P, HALVES, BLOCKS, HALF], F32, name="qa", tag="w_bf", align_bytes=64)
        qab = [keep.tile([P, BLOCKS, HALF], F32, name=f"qab{h}") for h in range(HALVES)]
        for b in range(BLOCKS):
            for h in range(HALVES):
                nc.vector.tensor_copy(qa[:, h, b, :], react_t[b][:].indirect(piece(cha_t, h)))
            for h in range(HALVES):
                nc.vector.tensor_tensor(qab[h][:, b, :], react_t[b][:].indirect(piece(chb_t, h)), qa[:, h, b, :], ALU.add)
        q2_t = [bank(f"B{h}", f"q2_t{h}") for h in range(HALVES)]
        for h in range(HALVES):
            to_nodes(q2_t[h], fetched(qab[h]), True, False, squares[:PER_HALF])
            to_nodes(q2_t[h], own(react_t, h), False, False)
            to_nodes(q2_t[h], own(react_t, h), False, False)
            to_nodes(q2_t[h], fetched(qab[h]), False, True, squares[PER_HALF:])

        rows_t = bank("C0", "rows_t")
        turn(rows_t[:, 0:P], rows[:], True, True)
        neg = keep.tile([P, 64], F32, name="neg")
        nc.scalar.activation(neg[:], rows_t[:, 0:64], ACT.Copy, scale=-1.0)

        va = [bank(f"C{h}", f"va{h}") for h in range(HALVES)]
        num = [bank(f"D{h}", f"num{h}") for h in range(HALVES)]
        side = keep.tile([P, 2, HALVES, S], F32, name="side", tag="after")
        drop_q = [side[:, 0, h, :] for h in range(HALVES)]
        q_sq = [side[:, 1, h, :] for h in range(HALVES)]

        def fetch_volt(h, b, drop):
            va_s = keep.tile([P, HALF], F32, name=f"va_s{h}{b}")
            nc.vector.tensor_tensor(va_s[:], volt_t[b][:].indirect(piece(par_t, h)), drop[:, b * HALF : (b + 1) * HALF], ALU.add)
            return va_s

        def drop_rows(h):
            drop = keep.tile([P, S], F32, name=f"drop{h}")
            nc.scalar.copy(drop[:], va[h][:])
            return drop

        def reactive_drop(h):
            for c, ms in per_chunk(h):
                nc.scalar.activation(drop_q[h][:, ms], q2_t[h][:, ms], ACT.Copy, scale=neg[:, 32 + c : 33 + c])
            to_rows(va[h], drop_q[h], True, False)

        def fetch_load_a(h, pa):
            p2_t = bank(f"A{h}", f"p2_t{h}")
            to_nodes(p2_t, own(load, h), True, False)
            to_nodes(p2_t, own(load, h), False, False)
            for b in range(BLOCKS):
                nc.vector.tensor_copy(pa[:, b, :], load[b][:].indirect(piece(cha_t, h)))
            return p2_t

        def fetch_load_b(h, pa, pab, p2_t):
            for b in range(BLOCKS):
                nc.vector.tensor_tensor(pab[:, b, :], load[b][:].indirect(piece(chb_t, h)), pa[:, b, :], ALU.add)
            to_nodes(p2_t, fetched(pab), False, True)

        def active_drop(h, p2_t):
            drop_p = keep.tile([P, S], F32, name=f"drop_p{h}", tag=f"drop_p{h}")
            for c, ms in per_chunk(h):
                nc.scalar.activation(drop_p[:, ms], p2_t[:, ms], ACT.Copy, scale=neg[:, c : c + 1])
            to_rows(va[h], drop_p, False, True)
            return drop_p

        def inverse(h, b, va_s):
            va_abs = keep.tile([P, HALF], F32, name=f"va_abs{h}{b}")
            root = keep.tile([P, HALF], F32, name=f"root{h}{b}")
            inv = keep.tile([P, HALF], F32, name=f"inv{h}{b}")
            nc.scalar.activation(va_abs[:], va_s[:], ACT.Abs)
            nc.scalar.activation(root[:], va_abs[:], ACT.Abs_reciprocal_sqrt, bias=0.3)
            nc.scalar.activation(inv[:], root[:], ACT.Square)
            return inv

        def active_loss(h, p2_t, drop_p):
            loss_p = keep.tile([P, S], F32, name=f"loss_p{h}")
            nc.vector.scalar_tensor_tensor(loss_p[:], p2_t[:], 0.25, drop_p[:], ALU.mult, ALU.mult)
            return loss_p

        def numerator(h, loss_p, loss):
            for c, ms in per_chunk(h):
                nc.vector.scalar_tensor_tensor(loss[:, ms], q_sq[h][:, ms], neg[:, c : c + 1], loss_p[:, ms], ALU.mult, ALU.add)
            to_rows(num[h], loss, True, True)

        def finish(h, b, inv):
            result = keep.tile([P, HALF], F32, name=f"result{h}{b}")
            nc.vector.scalar_tensor_tensor(result[:], num[h][:, b * HALF : (b + 1) * HALF], -1.0, inv[:], ALU.mult, ALU.mult)
            nc.sync.dma_start(out[b * P : (b + 1) * P, h * HALF : (h + 1) * HALF], result[:])

        p2_t = []
        drop_p = []
        drop = []
        for h in range(HALVES):
            reactive_drop(h)
            nc.scalar.activation(q_sq[h], q2_t[h][:], ACT.Square, scale=0.5)
            pa = keep.tile([P, BLOCKS, HALF], F32, name=f"pa{h}")
            pab = keep.tile([P, BLOCKS, HALF], F32, name=f"pab{h}", tag="pab")
            p2_t.append(fetch_load_a(h, pa))
            fetch_load_b(h, pa, pab, p2_t[h])
            drop_p.append(active_drop(h, p2_t[h]))
            drop.append(drop_rows(h))
        for h in range(HALVES):
            loss = keep.tile([P, S], F32, name=f"loss{h}")
            numerator(h, active_loss(h, p2_t[h], drop_p[h]), loss)
            inv = [inverse(h, b, fetch_volt(h, b, drop[h])) for b in range(BLOCKS)]
            for b in range(BLOCKS):
                finish(h, b, inv[b])
